import numpy as np
import ml_dtypes


def mxq(x, axis, fmt="e4m3"):
    dtype, down = {"e4m3": (ml_dtypes.float8_e4m3fn, 7), "e5m2": (ml_dtypes.float8_e5m2, 14)}[fmt]
    v = np.moveaxis(np.asarray(x, np.float32).astype(ml_dtypes.bfloat16).astype(np.float64), axis, -1)
    blocks = v.reshape(v.shape[:-1] + (-1, 32))
    amax = np.abs(blocks).max(-1, keepdims=True)
    byte = np.maximum(np.where(amax > 0, np.frexp(amax)[1] - 1 + 127, 0) - down, 1)
    scale = np.exp2(byte - 127.0)
    codes = (blocks / scale).astype(np.float32).astype(dtype).astype(np.float64)
    return np.moveaxis((codes * scale).reshape(v.shape), -1, axis)


WIDE = False


def mx_kscale(k):
    if not WIDE:
        return np.ones(k)
    levels = np.array([10, -10, 5, -5, 0])
    if k % 512:
        return np.exp2(np.random.permutation(np.resize(levels, k // 32))).repeat(32)
    a = np.empty((k // 512, 16))
    for p in range(k // 512):
        a[p, :8] = np.random.permutation(np.resize(levels, 8))
        for g in range(8):
            far = levels[np.abs(levels - a[p, g]) >= 10]
            a[p, g + 8] = far[np.random.randint(len(far))]
    return np.exp2(a.ravel()).repeat(32)


def f64(x):
    return np.asarray(x).astype(np.float64)


def striped(idx):
    return np.tile(np.asarray(idx).reshape(-1, 16).T, (8, 1)).astype(np.uint16)


def unstriped(offs):
    return offs[:16].T.reshape(-1).astype(np.int64)


E2M1 = np.array([0.0, 0.5, 1.0, 1.5, 2.0, 3.0, 4.0, 6.0, -0.0, -0.5, -1.0, -1.5, -2.0, -3.0, -4.0, -6.0])


def pack_weight(w, fmt):
    k, n = w.shape
    w = f64(np.asarray(w, np.float32).astype(ml_dtypes.bfloat16)).reshape(k // 32, 32, n)
    amax = np.abs(w).max(1)
    if fmt == "e4m3":
        byte = np.frexp(amax)[1] - 1 + 127 - 7
    else:
        mant, ex = np.frexp(amax / 6.0)
        byte = np.where(mant > 0.5, ex, ex - 1) + 127
    byte = np.clip(np.where(amax > 0, byte, 1), 1, 254)
    scaled = (w * np.exp2(127.0 - byte)[:, None, :]).reshape(k, n).astype(np.float32)
    by_word = np.ascontiguousarray(scaled.reshape(k // 512, 128, 4, n).transpose(0, 1, 3, 2))
    if fmt == "e4m3":
        words = by_word.astype(ml_dtypes.float8_e4m3fn).view(np.uint8)
    else:
        c = by_word.astype(ml_dtypes.float4_e2m1fn).view(np.uint8) & 0xF
        words = (c[..., 0::2] | (c[..., 1::2] << 4)).reshape(k // 512, 128, 2 * n)
    return np.ascontiguousarray(words), np.ascontiguousarray(byte.astype(np.uint8).reshape(k // 512, 16, n))


def unpack_weight(words, scales, fmt):
    g, _, n = scales.shape
    words = np.ascontiguousarray(words).reshape(g, 128, n, -1)
    if fmt == "e4m3":
        vals = words.view(ml_dtypes.float8_e4m3fn).astype(np.float64)
    else:
        nib = np.empty((g, 128, n, 4), np.uint8)
        nib[..., 0::2] = words & 0xF
        nib[..., 1::2] = words >> 4
        vals = E2M1[nib]
    vals = vals * np.repeat(np.exp2(scales.astype(np.float64) - 127.0), 8, axis=1)[..., None]
    return vals.transpose(0, 1, 3, 2).reshape(g * 512, n)


K, R, F, T, J, M = 512, 128, 512, 2048, 512, 256


def setup_inputs():
    n = np.random.standard_normal
    idx = np.random.permutation(T)[:J]
    idx2 = np.random.permutation(J)[:M]
    idx3 = np.random.permutation(J)[:M]
    fk = mx_kscale(K)
    ff = mx_kscale(F)
    fj = mx_kscale(J)
    tj = np.ones(T)
    tj[idx] = fj
    tabp = pack_weight(n((K, T)) / fk[:, None], "e2m1")
    return {
        "tab_words": tabp[0],
        "tab_scales": tabp[1],
        "w1": (n((K, R)) * 1 / np.sqrt(K) * fk[:, None]).astype(np.float32),
        "soft": (np.random.uniform(0.5, 1.5, (R, 1))).astype(np.float32),
        "wo": (n((F, R)) * 1 / np.sqrt(F) * ff[:, None]).astype(np.float32),
        "dy": (n((F, M)) / ff[:, None]).astype(np.float32),
        "js": (np.random.uniform(0.5, 2.0, (1, J)) * fj).astype(np.float32),
        "xrows": (n((K, T)) / tj).astype(np.float32),
        "old": (n((K, R)) * 4.0).astype(np.float32),
        "offs": striped(idx),
        "offs2": striped(idx2),
        "offs3": striped(idx3),
    }


def reference(tab_words, tab_scales, w1, soft, wo, dy, js, xrows, old, offs, offs2, offs3):
    idx = unstriped(offs)
    idx2 = unstriped(offs2)
    idx3 = unstriped(offs3)
    tabu = unpack_weight(tab_words, tab_scales, "e2m1")
    w1q = mxq(f64(w1), 0, "e4m3")
    tabidxg = tabu[:, idx]
    a = w1q.T @ tabidxg
    n2 = np.sqrt(np.square(a[:, idx2]) * np.square(a[:, idx3]) + f64(soft))
    woq = mxq(f64(wo), 0, "e4m3")
    dyq = mxq(f64(dy), 0, "e4m3")
    c0 = woq.T @ dyq
    dn2 = c0 * a[:, idx2] * a[:, idx3] / np.square(n2) * (-1.0)
    e1 = c0 / n2 * a[:, idx3]
    s1 = np.zeros((R, J))
    s1[:, idx2] = e1
    e2 = dn2 * 0.5 / np.sqrt(np.square(a[:, idx2]) * np.square(a[:, idx3]) + f64(soft)) * np.square(a[:, idx3]) * a[:, idx2] * 2.0
    s2 = np.zeros((R, J))
    s2[:, idx2] = e2
    e3 = c0 / n2 * a[:, idx2]
    s3 = np.zeros((R, J))
    s3[:, idx3] = e3
    e4 = dn2 * 0.5 / np.sqrt(np.square(a[:, idx2]) * np.square(a[:, idx3]) + f64(soft)) * np.square(a[:, idx2]) * a[:, idx3] * 2.0
    s4 = np.zeros((R, J))
    s4[:, idx3] = e4
    da = s1 + s2 + s3 + s4
    gs = da * f64(js)
    gt1 = gs.T
    xt = f64(xrows)[:, idx].T
    xtq = mxq(xt, 0, "e4m3")
    gt1q = mxq(gt1, 0, "e4m3")
    gw = xtq.T @ gt1q
    y = gw + f64(old)
    return y

@@ -1,0 +1,185 @@
+from contextlib import ExitStack
+
+import concourse.mybir as mybir
+from concourse.masks import make_identity
+
+K, R, F, T, J, M = 512, 128, 512, 2048, 512, 256
+P = 128
+PACK = 4
+FLOPS = 2 * K * R * J + 2 * F * R * M + 2 * J * K * R
+
+F32 = mybir.dt.float32
+BF16 = mybir.dt.bfloat16
+I32 = mybir.dt.int32
+U32 = mybir.dt.uint32
+U16 = mybir.dt.uint16
+U8 = mybir.dt.uint8
+FP8X4 = mybir.dt.float8_e4m3fn_x4
+FP4X4 = mybir.dt.float4_e2m1fn_x4
+ACT = mybir.ActivationFunctionType
+MULT = mybir.AluOpType.mult
+ADD = mybir.AluOpType.add
+
+
+def tile_attend_clikeness_w_kernel(tc, tab_words, tab_scales, w1, soft, wo, dy, js, xrows, old, offs, offs2, offs3, out):
+    nc = tc.nc
+    with ExitStack() as ctx:
+        lists = ctx.enter_context(tc.tile_pool(name="lists", bufs=1))
+        sb = ctx.enter_context(tc.tile_pool(name="sb", bufs=1))
+        ps = ctx.enter_context(tc.psum_pool(name="ps", bufs=1))
+
+        def tile(name, shape, dtype, after=None):
+            return sb.tile(shape, dtype, name=name, tag=after or name, align_bytes=64)
+
+        idx = lists.tile([P, J // 16], U16, name="idx")
+        idx2 = lists.tile([P, M // 16], U16, name="idx2")
+        idx3 = lists.tile([P, M // 16], U16, name="idx3")
+
+        tab_w = tile("tab_w", [P, T], U16)
+        tab_s = tile("tab_s", [P, T], U8)
+        w1_raw = tile("w1_raw", [P, PACK, R], F32)
+        wo_raw = tile("wo_raw", [P, PACK, R], F32)
+        dy_raw = tile("dy_raw", [P, PACK, M], F32)
+        old_sb = tile("old_sb", [P, PACK, R], F32)
+        soft_sb = tile("soft_sb", [P, 1], F32)
+        js_sb = tile("js_sb", [P, PACK], F32)
+        x_sb = [tile("x_sb%d" % c, [P, T], F32) for c in range(PACK)]
+        x_rows = xrows.rearrange("(p c) t -> p c t", c=PACK)
+
+        nc.gpsimd.memset(tab_s[:].bitcast(I32), 0)
+        nc.sync.dma_start(idx[:], offs)
+        for q in range(4):
+            nc.sync.dma_start(tab_s[32 * q : 32 * q + 4, :].bitcast(I32), tab_scales[0, 4 * q : 4 * q + 4, :].bitcast(I32))
+        nc.sync.dma_start(tab_w[:].bitcast(I32), tab_words[0].bitcast(I32))
+        nc.sync.dma_start(w1_raw[:], w1.rearrange("(p t) r -> p t r", t=PACK))
+        nc.sync.dma_start(wo_raw[:], wo.rearrange("(p t) r -> p t r", t=PACK))
+        nc.sync.dma_start(dy_raw[:], dy.rearrange("(p t) m -> p t m", t=PACK))
+        nc.sync.dma_start(idx2[:], offs2)
+        nc.sync.dma_start(idx3[:], offs3)
+        nc.sync.dma_start(x_sb[0][:], x_rows[:, 0, :])
+        nc.sync.dma_start(soft_sb[:], soft)
+        for c in range(1, PACK):
+            nc.sync.dma_start(x_sb[c][:], x_rows[:, c, :])
+        nc.sync.dma_start(js_sb[:], js.rearrange("o (p t) -> (o p) t", t=PACK))
+        nc.sync.dma_start(old_sb[:], old.rearrange("(p c) r -> p c r", c=PACK))
+
+        warm_in = tile("warm_in", [P, 1], F32)
+        warm_out = tile("warm_out", [P, 1], F32)
+        nc.vector.memset(warm_in[:], 1.0)
+        nc.scalar.activation(warm_out[:], warm_in[:], ACT.Abs_reciprocal_sqrt)
+
+        ident = tile("ident", [P, P], F32)
+        make_identity(nc, ident[:])
+        da2 = tile("da2", [P, J], F32)
+        da3 = tile("da3", [P, J], F32)
+        nc.vector.memset(da2[:], 0.0)
+        nc.vector.memset(da3[:], 0.0)
+
+        def quantise(name, grouped, width, after=None):
+            codes = tile(name + "_codes", [P, width], U32, after)
+            scales = tile(name + "_scales", [P, width], U8)
+            nc.vector.quantize_mx(out=codes[:].bitcast(FP8X4), scales=scales[:], in_=grouped)
+            return codes, scales
+
+        def interleave(copy, name, raw, width, after=None):
+            grouped = tile(name + "_grouped", [P, width, PACK], BF16, after)
+            copy(grouped[:], raw[:].rearrange("p t w -> p w t"))
+            return grouped[:].rearrange("p w t -> p (w t)")
+
+        def turn_x(picked, bank, grouped):
+            words = picked[:].bitcast(F32)
+            turned = ps.tile([P, 2, P], F32, name="x_turned", tag=bank)
+            for u in range(2):
+                nc.tensor.transpose(turned[:, u, :], words[:, u : J // 2 : 2], ident[:])
+            nc.scalar.copy(grouped.bitcast(F32).rearrange("p (k u) -> p k u", u=2), turned[:].rearrange("p u k -> p k u"))
+
+        def pick_x(c, after=None):
+            picked = tile("x_picked%d" % c, [P, J], BF16, after)
+            nc.vector.tensor_copy(picked[:], x_sb[c][:].indirect(idx[:]))
+            return picked
+
+        tab_wg = tile("tab_wg", [P, J], U16)
+        tab_sg = tile("tab_sg", [P, J], U8)
+        w1_grouped = interleave(nc.scalar.copy, "w1", w1_raw, R)
+        nc.vector.tensor_copy(tab_sg[:], tab_s[:].indirect(idx[:]))
+        nc.vector.tensor_copy(tab_wg[:], tab_w[:].indirect(idx[:]))
+        w1_codes, w1_scales = quantise("w1", w1_grouped, R)
+        a_ps = ps.tile([P, J], F32, name="a_ps", tag="bank_a")
+        nc.tensor.matmul_mx(out=a_ps[:], lhsT=w1_codes[:].bitcast(FP8X4), lhsT_scale=w1_scales[:],
+                            rhs=tab_wg[:].bitcast(FP4X4), rhs_scale=tab_sg[:], start=True, stop=True)
+        a_sb = tile("a_sb", [P, J], F32)
+        nc.scalar.copy(a_sb[:], a_ps[:])
+
+        wo_grouped = interleave(nc.vector.tensor_copy, "wo", wo_raw, R, "tab_s")
+        dy_grouped = interleave(nc.vector.tensor_copy, "dy", dy_raw, M, "w1_grouped")
+        wo_codes, wo_scales = quantise("wo", wo_grouped, R)
+        dy_codes, dy_scales = quantise("dy", dy_grouped, M)
+        c_ps = ps.tile([P, M], F32, name="c_ps", tag="bank_c")
+        nc.tensor.matmul_mx(out=c_ps[:], lhsT=wo_codes[:].bitcast(FP8X4), lhsT_scale=wo_scales[:],
+                            rhs=dy_codes[:].bitcast(FP8X4), rhs_scale=dy_scales[:], start=True, stop=True)
+
+        u_sb = tile("u_sb", [P, M], F32, "tab_s")
+        v_sb = tile("v_sb", [P, M], F32, "w1_grouped")
+        nc.vector.tensor_copy(u_sb[:], a_sb[:].indirect(idx2[:]))
+        nc.vector.tensor_copy(v_sb[:], a_sb[:].indirect(idx3[:]))
+        u2 = tile("u2", [P, M], F32)
+        v2 = tile("v2", [P, M], F32)
+        nc.scalar.activation(u2[:], u_sb[:], ACT.Square)
+        nc.scalar.activation(v2[:], v_sb[:], ACT.Square)
+
+        x01_grouped = tile("x01_grouped", [P, 2 * J], BF16)
+        x2_grouped = tile("x2_grouped", [P, J], BF16)
+        x3_grouped = tile("x3_grouped", [P, J], BF16)
+        picked0 = pick_x(0, "a_sb")
+        uv2 = tile("uv2", [P, M], F32, "x_sb0")
+        nc.vector.tensor_tensor(uv2[:], u2[:], v2[:], MULT)
+        rn = tile("rn", [P, M], F32)
+        nc.scalar.activation(rn[:], uv2[:], ACT.Abs_reciprocal_sqrt, bias=soft_sb[:])
+        rn2 = tile("rn2", [P, M], F32)
+        nc.scalar.activation(rn2[:], rn[:], ACT.Square)
+        picked1 = pick_x(1, "u2")
+        turn_x(picked0, "bank_x0", x01_grouped[:, :J])
+        turn_x(picked1, "bank_x1", x01_grouped[:, J:])
+
+        crn = tile("crn", [P, M], F32, "x_sb1")
+        nc.vector.scalar_tensor_tensor(crn[:], c_ps[:], soft_sb[:], rn[:], MULT, MULT)
+        wgt = tile("wgt", [P, M], F32)
+        nc.vector.tensor_tensor(wgt[:], crn[:], rn2[:], MULT)
+        nc.vector.tensor_tensor(da2[:].indirect(idx2[:]), wgt[:], v_sb[:], MULT)
+        nc.vector.tensor_tensor(da3[:].indirect(idx3[:]), wgt[:], u_sb[:], MULT)
+        x01_codes, x01_scales = quantise("x01", x01_grouped[:], 2 * P, "w1_grouped")
+
+        da_ps = ps.tile([P, PACK, R], F32, name="da_ps", tag="bank_da")
+        for s, src in enumerate((da2, da3)):
+            for t in range(PACK):
+                nc.tensor.matmul(da_ps[:, t, :], src[:, t:J:PACK], ident[:], start=(s == 0 and t == 0),
+                                 stop=(s == 1 and t == PACK - 1), is_transpose=True)
+
+        x2_bf = tile("x2_bf", [P, T], BF16, "rn")
+        nc.scalar.activation(x2_bf[:], x_sb[2][:], ACT.Copy)
+        picked2 = tile("x_picked2", [P, J], BF16, "da2")
+        nc.scalar.activation(picked2[:], x2_bf[:].indirect(idx[:]), ACT.Copy)
+
+        picked3 = pick_x(3, "wgt")
+        turn_x(picked2, "bank_x0", x2_grouped[:])
+        turn_x(picked3, "bank_x1", x3_grouped[:])
+
+        g_grouped = tile("g_grouped", [P, R, PACK], BF16, "x_sb3")
+        nc.vector.tensor_tensor(g_grouped[:], da_ps[:].rearrange("p t r -> p r t"),
+                                js_sb[:].unsqueeze(1).to_broadcast([P, R, PACK]), MULT)
+        g_codes, g_scales = quantise("g", g_grouped[:].rearrange("p r t -> p (r t)"), R)
+        x2_codes, x2_scales = quantise("x2", x2_grouped[:], P)
+        x3_codes, x3_scales = quantise("x3", x3_grouped[:], P)
+
+        res = tile("res", [P, PACK, R], F32)
+        out_rows = out.rearrange("(p c) r -> p c r", c=PACK)
+        x_q = [(x01_codes[:, :P], x01_scales[:, :P]), (x01_codes[:, P:], x01_scales[:, P:]),
+               (x2_codes[:], x2_scales[:]), (x3_codes[:], x3_scales[:])]
+        for lo, n, bank in ((0, 2, "bank_a"), (2, 1, "bank_c"), (3, 1, "bank_g")):
+            gw_ps = ps.tile([P, n, R], F32, name="gw_ps", tag=bank)
+            for i in range(n):
+                codes, scales = x_q[lo + i]
+                nc.tensor.matmul_mx(out=gw_ps[:, i, :], lhsT=codes.bitcast(FP8X4), lhsT_scale=scales,
+                                    rhs=g_codes[:].bitcast(FP8X4), rhs_scale=g_scales[:], start=True, stop=True)
+            nc.vector.tensor_tensor(res[:, lo : lo + n, :], gw_ps[:], old_sb[:, lo : lo + n, :], ADD)
+            nc.sync.dma_start(out_rows[:, lo : lo + n, :], res[:, lo : lo + n, :])

@@ -81,16 +81,20 @@ def tile_attend_clikeness_w_kernel(tc, tab_words, tab_scales, w1, soft, wo, dy, 
             nc.vector.quantize_mx(out=codes[:].bitcast(FP8X4), scales=scales[:], in_=grouped)
             return codes, scales
 
-        def interleave(copy, name, raw, width, after=None):
-            grouped = tile(name + "_grouped", [P, width, PACK], BF16, after)
-            copy(grouped[:], raw[:].rearrange("p t w -> p w t"))
+        def interleave(copy, grouped, raw):
+            copy(grouped.rearrange("p (c i) t -> p c t i", i=4), raw.rearrange("p t (c i) -> p c t i", i=4))
+
+        def flat(grouped):
             return grouped[:].rearrange("p w t -> p (w t)")
 
-        def turn_x(picked, bank, grouped):
+        def turn_x(picked, bank):
             words = picked[:].bitcast(F32)
             turned = ps.tile([P, 2, P], F32, name="x_turned", tag=bank)
             for u in range(2):
                 nc.tensor.transpose(turned[:, u, :], words[:, u : J // 2 : 2], ident[:])
+            return turned
+
+        def weave_x(grouped, turned):
             nc.scalar.copy(grouped.bitcast(F32).rearrange("p (k u) -> p k u", u=2), turned[:].rearrange("p u k -> p k u"))
 
         def pick_x(c, after=None):
@@ -100,54 +104,73 @@ def tile_attend_clikeness_w_kernel(tc, tab_words, tab_scales, w1, soft, wo, dy, 
 
         tab_wg = tile("tab_wg", [P, J], U16)
         tab_sg = tile("tab_sg", [P, J], U8)
-        w1_grouped = interleave(nc.scalar.copy, "w1", w1_raw, R)
-        nc.vector.tensor_copy(tab_sg[:], tab_s[:].indirect(idx[:]))
+        w1_grouped = tile("w1_grouped", [P, R, PACK], BF16)
+        wo_grouped = tile("wo_grouped", [P, R, PACK], BF16)
+        interleave(nc.scalar.copy, w1_grouped[:], w1_raw[:])
+        interleave(nc.scalar.copy, wo_grouped[:], wo_raw[:])
+        half = J // 2
         nc.vector.tensor_copy(tab_wg[:], tab_w[:].indirect(idx[:]))
-        w1_codes, w1_scales = quantise("w1", w1_grouped, R)
-        a_ps = ps.tile([P, J], F32, name="a_ps", tag="bank_a")
-        nc.tensor.matmul_mx(out=a_ps[:], lhsT=w1_codes[:].bitcast(FP8X4), lhsT_scale=w1_scales[:],
-                            rhs=tab_wg[:].bitcast(FP4X4), rhs_scale=tab_sg[:], start=True, stop=True)
-        a_sb = tile("a_sb", [P, J], F32)
-        nc.scalar.copy(a_sb[:], a_ps[:])
+        nc.vector.tensor_copy(tab_sg[:, :half], tab_s[:].indirect(idx[:, : half // 16]))
+        w1_codes, w1_scales = quantise("w1", flat(w1_grouped), R)
+        nc.vector.tensor_copy(tab_sg[:, half:], tab_s[:].indirect(idx[:, half // 16 :]))
+        a_ps = []
+        for h in range(2):
+            cols = slice(h * half, (h + 1) * half)
+            a_ps.append(ps.tile([P, half], F32, name="a_ps", tag="bank_a%d" % h))
+            nc.tensor.matmul_mx(out=a_ps[h][:], lhsT=w1_codes[:].bitcast(FP8X4), lhsT_scale=w1_scales[:],
+                                rhs=tab_wg[:, cols].bitcast(FP4X4), rhs_scale=tab_sg[:, cols], start=True, stop=True)
 
-        wo_grouped = interleave(nc.vector.tensor_copy, "wo", wo_raw, R, "tab_s")
-        dy_grouped = interleave(nc.vector.tensor_copy, "dy", dy_raw, M, "w1_grouped")
-        wo_codes, wo_scales = quantise("wo", wo_grouped, R)
-        dy_codes, dy_scales = quantise("dy", dy_grouped, M)
+        dy_grouped = tile("dy_grouped", [P, M, PACK], BF16, "w1_grouped")
+        interleave(nc.scalar.copy, dy_grouped[:, : M // 2, :], dy_raw[:, :, : M // 2])
+        interleave(nc.vector.tensor_copy, dy_grouped[:, M // 2 :, :], dy_raw[:, :, M // 2 :])
+        a_sb = tile("a_sb", [P, J], F32, "dy_raw")
+        for h in range(2):
+            nc.scalar.copy(a_sb[:, h * half : (h + 1) * half], a_ps[h][:])
+        wo_codes, wo_scales = quantise("wo", flat(wo_grouped), R, "tab_s")
+        dy_codes, dy_scales = quantise("dy", flat(dy_grouped), M)
         c_ps = ps.tile([P, M], F32, name="c_ps", tag="bank_c")
         nc.tensor.matmul_mx(out=c_ps[:], lhsT=wo_codes[:].bitcast(FP8X4), lhsT_scale=wo_scales[:],
                             rhs=dy_codes[:].bitcast(FP8X4), rhs_scale=dy_scales[:], start=True, stop=True)
 
-        u_sb = tile("u_sb", [P, M], F32, "tab_s")
-        v_sb = tile("v_sb", [P, M], F32, "w1_grouped")
+        u_sb = tile("u_sb", [P, M], F32)
+        v_sb = tile("v_sb", [P, M], F32)
         nc.vector.tensor_copy(u_sb[:], a_sb[:].indirect(idx2[:]))
         nc.vector.tensor_copy(v_sb[:], a_sb[:].indirect(idx3[:]))
-        u2 = tile("u2", [P, M], F32)
-        v2 = tile("v2", [P, M], F32)
-        nc.scalar.activation(u2[:], u_sb[:], ACT.Square)
-        nc.scalar.activation(v2[:], v_sb[:], ACT.Square)
+        def cast_x(c, after=None):
+            rounded = tile("x_bf%d" % c, [P, T], BF16, after)
+            nc.scalar.activation(rounded[:], x_sb[c][:], ACT.Copy)
+            return rounded
 
-        x01_grouped = tile("x01_grouped", [P, 2 * J], BF16)
-        x2_grouped = tile("x2_grouped", [P, J], BF16)
-        x3_grouped = tile("x3_grouped", [P, J], BF16)
-        picked0 = pick_x(0, "a_sb")
+        def pick_rounded_x(c, rounded, after):
+            picked = tile("x_picked%d" % c, [P, J], BF16, after)
+            nc.scalar.activation(picked[:], rounded[:].indirect(idx[:]), ACT.Copy)
+            return picked
+
+        x0_bf = cast_x(0)
+        cu = tile("cu", [P, M], F32)
+        cv = tile("cv", [P, M], F32)
+        uv = tile("uv", [P, M], F32)
+        nc.vector.scalar_tensor_tensor(cu[:], c_ps[:], soft_sb[:], u_sb[:], MULT, MULT)
+        nc.vector.tensor_tensor(uv[:], u_sb[:], v_sb[:], MULT)
+        nc.vector.scalar_tensor_tensor(cv[:], c_ps[:], soft_sb[:], v_sb[:], MULT, MULT)
         uv2 = tile("uv2", [P, M], F32, "x_sb0")
-        nc.vector.tensor_tensor(uv2[:], u2[:], v2[:], MULT)
+        nc.scalar.activation(uv2[:], uv[:], ACT.Square)
         rn = tile("rn", [P, M], F32)
         nc.scalar.activation(rn[:], uv2[:], ACT.Abs_reciprocal_sqrt, bias=soft_sb[:])
         rn2 = tile("rn2", [P, M], F32)
         nc.scalar.activation(rn2[:], rn[:], ACT.Square)
-        picked1 = pick_x(1, "u2")
-        turn_x(picked0, "bank_x0", x01_grouped[:, :J])
-        turn_x(picked1, "bank_x1", x01_grouped[:, J:])
+        picked1 = pick_x(1)
+        picked0 = pick_rounded_x(0, x0_bf, "x_sb0")
 
-        crn = tile("crn", [P, M], F32, "x_sb1")
-        nc.vector.scalar_tensor_tensor(crn[:], c_ps[:], soft_sb[:], rn[:], MULT, MULT)
-        wgt = tile("wgt", [P, M], F32)
-        nc.vector.tensor_tensor(wgt[:], crn[:], rn2[:], MULT)
-        nc.vector.tensor_tensor(da2[:].indirect(idx2[:]), wgt[:], v_sb[:], MULT)
-        nc.vector.tensor_tensor(da3[:].indirect(idx3[:]), wgt[:], u_sb[:], MULT)
-        x01_codes, x01_scales = quantise("x01", x01_grouped[:], 2 * P, "w1_grouped")
+        rvu = tile("rvu", [P, 2, M], F32, "x_sb1")
+        nc.vector.tensor_tensor(rvu[:, 0, :], cv[:], rn[:], MULT)
+        nc.vector.tensor_tensor(rvu[:, 1, :], cu[:], rn[:], MULT)
+        nc.vector.tensor_tensor(da2[:].indirect(idx2[:]), rvu[:, 0, :], rn2[:], MULT)
+        nc.vector.tensor_tensor(da3[:].indirect(idx3[:]), rvu[:, 1, :], rn2[:], MULT)
+        picked3 = pick_x(3)
+        x2_bf = cast_x(2, "x_bf0")
+        turned1 = turn_x(picked1, "bank_x1")
+        turned0 = turn_x(picked0, "bank_x0")
 
         da_ps = ps.tile([P, PACK, R], F32, name="da_ps", tag="bank_da")
         for s, src in enumerate((da2, da3)):
@@ -155,27 +178,30 @@ def tile_attend_clikeness_w_kernel(tc, tab_words, tab_scales, w1, soft, wo, dy, 
                 nc.tensor.matmul(da_ps[:, t, :], src[:, t:J:PACK], ident[:], start=(s == 0 and t == 0),
                                  stop=(s == 1 and t == PACK - 1), is_transpose=True)
 
-        x2_bf = tile("x2_bf", [P, T], BF16, "rn")
-        nc.scalar.activation(x2_bf[:], x_sb[2][:], ACT.Copy)
-        picked2 = tile("x_picked2", [P, J], BF16, "da2")
-        nc.scalar.activation(picked2[:], x2_bf[:].indirect(idx[:]), ACT.Copy)
-
-        picked3 = pick_x(3, "wgt")
-        turn_x(picked2, "bank_x0", x2_grouped[:])
-        turn_x(picked3, "bank_x1", x3_grouped[:])
+        picked2 = pick_rounded_x(2, x2_bf, "da2")
+        turned3 = turn_x(picked3, "bank_x3")
+        turned2 = turn_x(picked2, "bank_x2")
+        x01_grouped = tile("x01_grouped", [P, 2 * J], BF16, "x_bf0")
+        x2_grouped = tile("x2_grouped", [P, J], BF16)
+        x3_grouped = tile("x3_grouped", [P, J], BF16)
+        weave_x(x01_grouped[:, J:], turned1)
+        weave_x(x01_grouped[:, :J], turned0)
+        weave_x(x3_grouped[:], turned3)
+        weave_x(x2_grouped[:], turned2)
 
         g_grouped = tile("g_grouped", [P, R, PACK], BF16, "x_sb3")
         nc.vector.tensor_tensor(g_grouped[:], da_ps[:].rearrange("p t r -> p r t"),
                                 js_sb[:].unsqueeze(1).to_broadcast([P, R, PACK]), MULT)
-        g_codes, g_scales = quantise("g", g_grouped[:].rearrange("p r t -> p (r t)"), R)
-        x2_codes, x2_scales = quantise("x2", x2_grouped[:], P)
+        g_codes, g_scales = quantise("g", flat(g_grouped), R)
+        x01_codes, x01_scales = quantise("x01", x01_grouped[:], 2 * P, "js_sb")
         x3_codes, x3_scales = quantise("x3", x3_grouped[:], P)
+        x2_codes, x2_scales = quantise("x2", x2_grouped[:], P)
 
         res = tile("res", [P, PACK, R], F32)
         out_rows = out.rearrange("(p c) r -> p c r", c=PACK)
         x_q = [(x01_codes[:, :P], x01_scales[:, :P]), (x01_codes[:, P:], x01_scales[:, P:]),
                (x2_codes[:], x2_scales[:]), (x3_codes[:], x3_scales[:])]
-        for lo, n, bank in ((0, 2, "bank_a"), (2, 1, "bank_c"), (3, 1, "bank_g")):
+        for lo, n, bank in ((0, 2, "bank_a0"), (3, 1, "bank_a1"), (2, 1, "bank_c")):
             gw_ps = ps.tile([P, n, R], F32, name="gw_ps", tag=bank)
             for i in range(n):
                 codes, scales = x_q[lo + i]

from contextlib import ExitStack

import concourse.mybir as mybir
from concourse.masks import make_identity

K, R, F, T, J, M = 512, 128, 512, 2048, 512, 256
P = 128
PACK = 4
FLOPS = 2 * K * R * J + 2 * F * R * M + 2 * J * K * R

F32 = mybir.dt.float32
BF16 = mybir.dt.bfloat16
I32 = mybir.dt.int32
U32 = mybir.dt.uint32
U16 = mybir.dt.uint16
U8 = mybir.dt.uint8
FP8X4 = mybir.dt.float8_e4m3fn_x4
FP4X4 = mybir.dt.float4_e2m1fn_x4
ACT = mybir.ActivationFunctionType
MULT = mybir.AluOpType.mult
ADD = mybir.AluOpType.add


def tile_attend_clikeness_w_kernel(tc, tab_words, tab_scales, w1, soft, wo, dy, js, xrows, old, offs, offs2, offs3, out):
    nc = tc.nc
    with ExitStack() as ctx:
        lists = ctx.enter_context(tc.tile_pool(name="lists", bufs=1))
        sb = ctx.enter_context(tc.tile_pool(name="sb", bufs=1))
        ps = ctx.enter_context(tc.psum_pool(name="ps", bufs=1))

        def tile(name, shape, dtype, after=None):
            return sb.tile(shape, dtype, name=name, tag=after or name, align_bytes=64)

        idx = lists.tile([P, J // 16], U16, name="idx")
        idx2 = lists.tile([P, M // 16], U16, name="idx2")
        idx3 = lists.tile([P, M // 16], U16, name="idx3")

        tab_w = tile("tab_w", [P, T], U16)
        tab_s = tile("tab_s", [P, T], U8)
        w1_raw = tile("w1_raw", [P, PACK, R], F32)
        wo_raw = tile("wo_raw", [P, PACK, R], F32)
        dy_raw = tile("dy_raw", [P, PACK, M], F32)
        old_sb = tile("old_sb", [P, PACK, R], F32)
        soft_sb = tile("soft_sb", [P, 1], F32)
        js_sb = tile("js_sb", [P, PACK], F32)
        x_sb = [tile("x_sb%d" % c, [P, T], F32) for c in range(PACK)]
        x_rows = xrows.rearrange("(p c) t -> p c t", c=PACK)

        nc.gpsimd.memset(tab_s[:].bitcast(I32), 0)
        nc.sync.dma_start(idx[:], offs)
        for q in range(4):
            nc.sync.dma_start(tab_s[32 * q : 32 * q + 4, :].bitcast(I32), tab_scales[0, 4 * q : 4 * q + 4, :].bitcast(I32))
        nc.sync.dma_start(tab_w[:].bitcast(I32), tab_words[0].bitcast(I32))
        nc.sync.dma_start(w1_raw[:], w1.rearrange("(p t) r -> p t r", t=PACK))
        nc.sync.dma_start(wo_raw[:], wo.rearrange("(p t) r -> p t r", t=PACK))
        nc.sync.dma_start(dy_raw[:], dy.rearrange("(p t) m -> p t m", t=PACK))
        nc.sync.dma_start(idx2[:], offs2)
        nc.sync.dma_start(idx3[:], offs3)
        nc.sync.dma_start(x_sb[0][:], x_rows[:, 0, :])
        nc.sync.dma_start(soft_sb[:], soft)
        for c in range(1, PACK):
            nc.sync.dma_start(x_sb[c][:], x_rows[:, c, :])
        nc.sync.dma_start(js_sb[:], js.rearrange("o (p t) -> (o p) t", t=PACK))
        nc.sync.dma_start(old_sb[:], old.rearrange("(p c) r -> p c r", c=PACK))

        warm_in = tile("warm_in", [P, 1], F32)
        warm_out = tile("warm_out", [P, 1], F32)
        nc.vector.memset(warm_in[:], 1.0)
        nc.scalar.activation(warm_out[:], warm_in[:], ACT.Abs_reciprocal_sqrt)

        ident = tile("ident", [P, P], F32)
        make_identity(nc, ident[:])
        da2 = tile("da2", [P, J], F32)
        da3 = tile("da3", [P, J], F32)
        nc.vector.memset(da2[:], 0.0)
        nc.vector.memset(da3[:], 0.0)

        def quantise(name, grouped, width, after=None):
            codes = tile(name + "_codes", [P, width], U32, after)
            scales = tile(name + "_scales", [P, width], U8)
            nc.vector.quantize_mx(out=codes[:].bitcast(FP8X4), scales=scales[:], in_=grouped)
            return codes, scales

        def interleave(copy, grouped, raw):
            copy(grouped.rearrange("p (c i) t -> p c t i", i=4), raw.rearrange("p t (c i) -> p c t i", i=4))

        def flat(grouped):
            return grouped[:].rearrange("p w t -> p (w t)")

        def turn_x(picked, bank):
            words = picked[:].bitcast(F32)
            turned = ps.tile([P, 2, P], F32, name="x_turned", tag=bank)
            for u in range(2):
                nc.tensor.transpose(turned[:, u, :], words[:, u : J // 2 : 2], ident[:])
            return turned

        def weave_x(grouped, turned):
            nc.scalar.copy(grouped.bitcast(F32).rearrange("p (k u) -> p k u", u=2), turned[:].rearrange("p u k -> p k u"))

        def pick_x(c, after=None):
            picked = tile("x_picked%d" % c, [P, J], BF16, after)
            nc.vector.tensor_copy(picked[:], x_sb[c][:].indirect(idx[:]))
            return picked

        tab_wg = tile("tab_wg", [P, J], U16)
        tab_sg = tile("tab_sg", [P, J], U8)
        w1_grouped = tile("w1_grouped", [P, R, PACK], BF16)
        wo_grouped = tile("wo_grouped", [P, R, PACK], BF16)
        interleave(nc.scalar.copy, w1_grouped[:], w1_raw[:])
        interleave(nc.scalar.copy, wo_grouped[:], wo_raw[:])
        half = J // 2
        nc.vector.tensor_copy(tab_wg[:], tab_w[:].indirect(idx[:]))
        nc.vector.tensor_copy(tab_sg[:, :half], tab_s[:].indirect(idx[:, : half // 16]))
        w1_codes, w1_scales = quantise("w1", flat(w1_grouped), R)
        nc.vector.tensor_copy(tab_sg[:, half:], tab_s[:].indirect(idx[:, half // 16 :]))
        a_ps = []
        for h in range(2):
            cols = slice(h * half, (h + 1) * half)
            a_ps.append(ps.tile([P, half], F32, name="a_ps", tag="bank_a%d" % h))
            nc.tensor.matmul_mx(out=a_ps[h][:], lhsT=w1_codes[:].bitcast(FP8X4), lhsT_scale=w1_scales[:],
                                rhs=tab_wg[:, cols].bitcast(FP4X4), rhs_scale=tab_sg[:, cols], start=True, stop=True)

        dy_grouped = tile("dy_grouped", [P, M, PACK], BF16, "w1_grouped")
        interleave(nc.scalar.copy, dy_grouped[:, : M // 2, :], dy_raw[:, :, : M // 2])
        interleave(nc.vector.tensor_copy, dy_grouped[:, M // 2 :, :], dy_raw[:, :, M // 2 :])
        a_sb = tile("a_sb", [P, J], F32, "dy_raw")
        for h in range(2):
            nc.scalar.copy(a_sb[:, h * half : (h + 1) * half], a_ps[h][:])
        wo_codes, wo_scales = quantise("wo", flat(wo_grouped), R, "tab_s")
        dy_codes, dy_scales = quantise("dy", flat(dy_grouped), M)
        c_ps = ps.tile([P, M], F32, name="c_ps", tag="bank_c")
        nc.tensor.matmul_mx(out=c_ps[:], lhsT=wo_codes[:].bitcast(FP8X4), lhsT_scale=wo_scales[:],
                            rhs=dy_codes[:].bitcast(FP8X4), rhs_scale=dy_scales[:], start=True, stop=True)

        u_sb = tile("u_sb", [P, M], F32)
        v_sb = tile("v_sb", [P, M], F32)
        nc.vector.tensor_copy(u_sb[:], a_sb[:].indirect(idx2[:]))
        nc.vector.tensor_copy(v_sb[:], a_sb[:].indirect(idx3[:]))
        def cast_x(c, after=None):
            rounded = tile("x_bf%d" % c, [P, T], BF16, after)
            nc.scalar.activation(rounded[:], x_sb[c][:], ACT.Copy)
            return rounded

        def pick_rounded_x(c, rounded, after):
            picked = tile("x_picked%d" % c, [P, J], BF16, after)
            nc.scalar.activation(picked[:], rounded[:].indirect(idx[:]), ACT.Copy)
            return picked

        x0_bf = cast_x(0)
        cu = tile("cu", [P, M], F32)
        cv = tile("cv", [P, M], F32)
        uv = tile("uv", [P, M], F32)
        nc.vector.scalar_tensor_tensor(cu[:], c_ps[:], soft_sb[:], u_sb[:], MULT, MULT)
        nc.vector.tensor_tensor(uv[:], u_sb[:], v_sb[:], MULT)
        nc.vector.scalar_tensor_tensor(cv[:], c_ps[:], soft_sb[:], v_sb[:], MULT, MULT)
        uv2 = tile("uv2", [P, M], F32, "x_sb0")
        nc.scalar.activation(uv2[:], uv[:], ACT.Square)
        rn = tile("rn", [P, M], F32)
        nc.scalar.activation(rn[:], uv2[:], ACT.Abs_reciprocal_sqrt, bias=soft_sb[:])
        rn2 = tile("rn2", [P, M], F32)
        nc.scalar.activation(rn2[:], rn[:], ACT.Square)
        picked1 = pick_x(1)
        picked0 = pick_rounded_x(0, x0_bf, "x_sb0")

        rvu = tile("rvu", [P, 2, M], F32, "x_sb1")
        nc.vector.tensor_tensor(rvu[:, 0, :], cv[:], rn[:], MULT)
        nc.vector.tensor_tensor(rvu[:, 1, :], cu[:], rn[:], MULT)
        nc.vector.tensor_tensor(da2[:].indirect(idx2[:]), rvu[:, 0, :], rn2[:], MULT)
        nc.vector.tensor_tensor(da3[:].indirect(idx3[:]), rvu[:, 1, :], rn2[:], MULT)
        picked3 = pick_x(3)
        x2_bf = cast_x(2, "x_bf0")
        turned1 = turn_x(picked1, "bank_x1")
        turned0 = turn_x(picked0, "bank_x0")

        da_ps = ps.tile([P, PACK, R], F32, name="da_ps", tag="bank_da")
        for s, src in enumerate((da2, da3)):
            for t in range(PACK):
                nc.tensor.matmul(da_ps[:, t, :], src[:, t:J:PACK], ident[:], start=(s == 0 and t == 0),
                                 stop=(s == 1 and t == PACK - 1), is_transpose=True)

        picked2 = pick_rounded_x(2, x2_bf, "da2")
        turned3 = turn_x(picked3, "bank_x3")
        turned2 = turn_x(picked2, "bank_x2")
        x01_grouped = tile("x01_grouped", [P, 2 * J], BF16, "x_bf0")
        x2_grouped = tile("x2_grouped", [P, J], BF16)
        x3_grouped = tile("x3_grouped", [P, J], BF16)
        weave_x(x01_grouped[:, J:], turned1)
        weave_x(x01_grouped[:, :J], turned0)
        weave_x(x3_grouped[:], turned3)
        weave_x(x2_grouped[:], turned2)

        g_grouped = tile("g_grouped", [P, R, PACK], BF16, "x_sb3")
        nc.vector.tensor_tensor(g_grouped[:], da_ps[:].rearrange("p t r -> p r t"),
                                js_sb[:].unsqueeze(1).to_broadcast([P, R, PACK]), MULT)
        g_codes, g_scales = quantise("g", flat(g_grouped), R)
        x01_codes, x01_scales = quantise("x01", x01_grouped[:], 2 * P, "js_sb")
        x3_codes, x3_scales = quantise("x3", x3_grouped[:], P)
        x2_codes, x2_scales = quantise("x2", x2_grouped[:], P)

        res = tile("res", [P, PACK, R], F32)
        out_rows = out.rearrange("(p c) r -> p c r", c=PACK)
        x_q = [(x01_codes[:, :P], x01_scales[:, :P]), (x01_codes[:, P:], x01_scales[:, P:]),
               (x2_codes[:], x2_scales[:]), (x3_codes[:], x3_scales[:])]
        for lo, n, bank in ((0, 2, "bank_a0"), (3, 1, "bank_a1"), (2, 1, "bank_c")):
            gw_ps = ps.tile([P, n, R], F32, name="gw_ps", tag=bank)
            for i in range(n):
                codes, scales = x_q[lo + i]
                nc.tensor.matmul_mx(out=gw_ps[:, i, :], lhsT=codes.bitcast(FP8X4), lhsT_scale=scales,
                                    rhs=g_codes[:].bitcast(FP8X4), rhs_scale=g_scales[:], start=True, stop=True)
            nc.vector.tensor_tensor(res[:, lo : lo + n, :], gw_ps[:], old_sb[:, lo : lo + n, :], ADD)
            nc.sync.dma_start(out_rows[:, lo : lo + n, :], res[:, lo : lo + n, :])
